import numpy as np
import ml_dtypes


def mxq(x, axis, fmt="e4m3"):
    dtype, down = {"e4m3": (ml_dtypes.float8_e4m3fn, 7), "e5m2": (ml_dtypes.float8_e5m2, 14)}[fmt]
    v = np.moveaxis(np.asarray(x, np.float32).astype(ml_dtypes.bfloat16).astype(np.float64), axis, -1)
    blocks = v.reshape(v.shape[:-1] + (-1, 32))
    amax = np.abs(blocks).max(-1, keepdims=True)
    byte = np.maximum(np.where(amax > 0, np.frexp(amax)[1] - 1 + 127, 0) - down, 1)
    scale = np.exp2(byte - 127.0)
    codes = (blocks / scale).astype(np.float32).astype(dtype).astype(np.float64)
    return np.moveaxis((codes * scale).reshape(v.shape), -1, axis)


WIDE = False


def mx_kscale(k):
    if not WIDE:
        return np.ones(k)
    levels = np.array([10, -10, 5, -5, 0])
    if k % 512:
        return np.exp2(np.random.permutation(np.resize(levels, k // 32))).repeat(32)
    a = np.empty((k // 512, 16))
    for p in range(k // 512):
        a[p, :8] = np.random.permutation(np.resize(levels, 8))
        for g in range(8):
            far = levels[np.abs(levels - a[p, g]) >= 10]
            a[p, g + 8] = far[np.random.randint(len(far))]
    return np.exp2(a.ravel()).repeat(32)


BF16 = ml_dtypes.bfloat16


def bf(x):
    return np.asarray(x, np.float32).astype(BF16)


def f64(x):
    return np.asarray(x).astype(np.float64)


E2M1 = np.array([0.0, 0.5, 1.0, 1.5, 2.0, 3.0, 4.0, 6.0, -0.0, -0.5, -1.0, -1.5, -2.0, -3.0, -4.0, -6.0])


def pack_weight(w, fmt):
    k, n = w.shape
    w = f64(bf(w)).reshape(k // 32, 32, n)
    amax = np.abs(w).max(1)
    if fmt == "e4m3":
        byte = np.frexp(amax)[1] - 1 + 127 - 7
    else:
        mant, ex = np.frexp(amax / 6.0)
        byte = np.where(mant > 0.5, ex, ex - 1) + 127
    byte = np.clip(np.where(amax > 0, byte, 1), 1, 254)
    scaled = (w * np.exp2(127.0 - byte)[:, None, :]).reshape(k, n).astype(np.float32)
    by_word = np.ascontiguousarray(scaled.reshape(k // 512, 128, 4, n).transpose(0, 1, 3, 2))
    if fmt == "e4m3":
        words = by_word.astype(ml_dtypes.float8_e4m3fn).view(np.uint8)
    else:
        c = by_word.astype(ml_dtypes.float4_e2m1fn).view(np.uint8) & 0xF
        words = c[..., 0::2] | (c[..., 1::2] << 4)
    return np.ascontiguousarray(words), np.ascontiguousarray(byte.astype(np.uint8).reshape(k // 512, 16, n))


def unpack_weight(words, scales, fmt):
    g, p, n, _ = words.shape
    if fmt == "e4m3":
        vals = np.ascontiguousarray(words).view(ml_dtypes.float8_e4m3fn).astype(np.float64)
    else:
        nib = np.empty((g, p, n, 4), np.uint8)
        nib[..., 0::2] = words & 0xF
        nib[..., 1::2] = words >> 4
        vals = E2M1[nib]
    vals = vals * np.repeat(np.exp2(scales.astype(np.float64) - 127.0), 8, axis=1)[..., None]
    return vals.transpose(0, 1, 3, 2).reshape(g * 512, n)
def pack4(w):
    words, scales = pack_weight(w, "e2m1")
    return words.reshape(words.shape[0], 128, -1), scales


def unpack4(words, scales):
    return unpack_weight(words.reshape(words.shape[0], 128, -1, 2), scales, "e2m1")


B, T, D, M, Z = 4, 1024, 1024, 512, 512


def setup_inputs():
    s = mx_kscale(B * D).reshape(B, D)
    t = mx_kscale(B * M).reshape(B, M)
    drive = np.random.standard_normal((B, T, D)) * s[:, None, :]
    src = np.random.standard_normal((B, D, M)) / np.sqrt(D) / s[:, :, None] * t[:, None, :]
    rcv = np.random.standard_normal((B, M, Z)) / np.sqrt(M) / t[:, :, None]
    src_words, src_scales = pack4(src.reshape(B * D, M))
    rcv_words, rcv_scales = pack4(rcv.reshape(B * M, Z))
    return {"drive": bf(drive),
            "src_words": src_words,
            "src_scales": src_scales,
            "decay": bf(-0.1 - 0.9 * np.random.random_sample((B, M))),
            "dist": bf(0.2 + 1.8 * np.random.random_sample(T)),
            "rcv_words": rcv_words,
            "rcv_scales": rcv_scales}


def reference(drive, src_words, src_scales, decay, dist, rcv_words, rcv_scales):
    src = unpack4(src_words, src_scales).reshape(B, D, M)
    rcv = unpack4(rcv_words, rcv_scales).reshape(B, M, Z)
    amp = mxq(f64(drive), 2, "e4m3") @ src
    loss = np.exp(f64(dist)[None, :, None] * f64(decay)[:, None, :])
    far = amp * loss
    return mxq(far, 2, "e4m3") @ rcv

@@ -1,0 +1,278 @@
+from contextlib import ExitStack
+
+import concourse.mybir as mybir
+from concourse.masks import make_identity
+
+B, T, D, M, Z = 4, 1024, 1024, 512, 512
+FLOPS = 2 * B * T * (D * M + M * Z)
+
+F32 = mybir.dt.float32
+BF16 = mybir.dt.bfloat16
+I32 = mybir.dt.int32
+U32 = mybir.dt.uint32
+U8 = mybir.dt.uint8
+FP8X4 = mybir.dt.float8_e4m3fn_x4
+FP4X4 = mybir.dt.float4_e2m1fn_x4
+EXP = mybir.ActivationFunctionType.Exp
+MULT = mybir.AluOpType.mult
+
+P = 128
+K_PASS = 512
+PASS_WORDS = K_PASS // 2
+SRC_PASSES = D // K_PASS
+ROWS = T // P
+TILES = B * ROWS
+SINGLES_HEAD = 2
+SINGLES_TAIL = 2
+SCALAR_EXTRA = 3
+LOSS_LEAD = 2
+DRIVE_LEAD = 1
+VECTOR_HEAD = 2
+
+
+def tile_normal_mode_field_s14_kernel(
+    tc, drive, src_words, src_scales, decay, dist, rcv_words, rcv_scales, out
+):
+    nc = tc.nc
+    steps = [[i] for i in range(SINGLES_HEAD)]
+    steps = steps + [[i, i + 1] for i in range(SINGLES_HEAD, TILES - SINGLES_TAIL, 2)]
+    steps = steps + [[i] for i in range(TILES - SINGLES_TAIL, TILES)]
+    with ExitStack() as ctx:
+        keep = ctx.enter_context(tc.tile_pool(name="keep", bufs=1))
+        work = ctx.enter_context(tc.tile_pool(name="work", bufs=3))
+        psum = ctx.enter_context(tc.psum_pool(name="psum", bufs=2))
+        ctx.enter_context(tc.manual_schedule())
+
+        ident = keep.tile([P, P], F32, name="ident")
+        make_identity(nc, ident[:])
+
+        def cleared_plane(passes, name):
+            plane = keep.tile([P, passes, M], U8, name=name, align_bytes=64)
+            nc.vector.memset(plane[:].bitcast(I32), 0)
+            return plane
+
+        first_plane = cleared_plane(SRC_PASSES, "first_plane")
+        rcv_plane = cleared_plane(B, "rcv_plane")
+        rest_plane = cleared_plane((B - 1) * SRC_PASSES, "rest_plane")
+        src_planes = [first_plane[:, g, :] for g in range(SRC_PASSES)]
+        src_planes = src_planes + [rest_plane[:, g, :] for g in range((B - 1) * SRC_PASSES)]
+
+        shots = drive.rearrange("b (p j) d -> b p j d", j=ROWS)
+        fields = out.rearrange("b (p j) z -> b p j z", j=ROWS)
+
+        drive_rows = {}
+
+        def load_drive(step):
+            band, row = divmod(steps[step][0], ROWS)
+            count = len(steps[step])
+            rows = keep.tile([P, count * D], BF16, name="drive%d" % step)
+            nc.sync.dma_start(
+                out=rows[:], in_=shots[band, :, row : row + count, :].rearrange("p j d -> p (j d)")
+            )
+            for a, i in enumerate(steps[step]):
+                drive_rows[i] = rows[:, a * D : (a + 1) * D]
+
+        def load_scales(plane, scales):
+            for r in range(4):
+                nc.sync.dma_start(
+                    out=plane[:].bitcast(I32)[r:P:32, :, :],
+                    in_=scales.bitcast(I32)[:, r:16:4, :].rearrange("g q n -> q g n"),
+                )
+
+        def load_words(words, first, count, name):
+            tile = keep.tile([P, count, 2 * M], U8, name=name, align_bytes=64)
+            nc.sync.dma_start(
+                out=tile[:].bitcast(I32),
+                in_=words.bitcast(I32)[first : first + count].rearrange("g p n -> p g n"),
+            )
+            return [tile[:, g, :] for g in range(count)]
+
+        def load_decay(first, count):
+            tile = keep.tile([P, count * M], BF16, name="decay%d" % first)
+            nc.sync.dma_start(
+                out=tile[:],
+                in_=decay[first : first + count].rearrange("b m -> (b m)").partition_broadcast(P),
+            )
+            return [tile[:, b * M : (b + 1) * M] for b in range(count)]
+
+        load_drive(0)
+        load_scales(first_plane, src_scales[:SRC_PASSES])
+        src_codes = load_words(src_words, 0, SRC_PASSES, "src_first")
+        load_drive(1)
+        dist_bf = keep.tile([P, ROWS], BF16, name="dist_bf")
+        nc.sync.dma_start(out=dist_bf[:], in_=dist.rearrange("(p j) -> p j", j=ROWS))
+        decay_rows = load_decay(0, 1)
+        load_drive(2)
+        load_drive(3)
+        load_scales(rcv_plane, rcv_scales)
+        rcv_codes = load_words(rcv_words, 0, B, "rcv_all")
+        load_drive(4)
+        load_scales(rest_plane, src_scales[SRC_PASSES:])
+        decay_rows = decay_rows + load_decay(1, B - 1)
+        load_drive(5)
+        src_codes = src_codes + load_words(src_words, SRC_PASSES, (B - 1) * SRC_PASSES, "src_rest")
+        for step in range(6, len(steps)):
+            load_drive(step)
+
+        dist_f32 = keep.tile([P, ROWS], F32, name="dist_f32")
+        nc.scalar.copy(out=dist_f32[:], in_=dist_bf[:])
+
+        t = {}
+
+        def turn_drive(i):
+            bank = psum.tile([P, 2 * SRC_PASSES, P], F32, name="turned_drive", bufs=3)
+            words = drive_rows[i].bitcast(F32)
+            for g in range(SRC_PASSES):
+                for u in range(2):
+                    nc.tensor.transpose(
+                        bank[:, 2 * g + u, :],
+                        words[:, g * PASS_WORDS + u : (g + 1) * PASS_WORDS : 2],
+                        ident[:],
+                    )
+            t["turned_drive", i] = bank
+
+        def copy(engine, out, in_):
+            if engine == "v":
+                nc.vector.tensor_copy(out=out, in_=in_)
+            else:
+                nc.scalar.copy(out=out, in_=in_)
+
+        def group_drive(step, a, engine):
+            if a == 0:
+                t["drive_k", step] = work.tile([P, len(steps[step]) * D], BF16, name="drive_k", align_bytes=64, bufs=4)
+            words = t["drive_k", step][:].bitcast(F32)[:, a * D // 2 : (a + 1) * D // 2]
+            copy(
+                engine,
+                words.rearrange("p (g r u) -> p g r u", g=SRC_PASSES, u=2),
+                t["turned_drive", steps[step][a]][:].rearrange("p (g u) r -> p g r u", u=2),
+            )
+
+        def quantize(key, step, depth):
+            width = depth * len(steps[step]) // 4
+            codes = work.tile([P, width], U32, name=key + "_codes", align_bytes=64)
+            scales = work.tile([P, width], U8, name=key + "_scales", align_bytes=64)
+            nc.vector.quantize_mx(out=codes[:].bitcast(FP8X4), scales=scales[:], in_=t[key, step][:])
+            t[key + "_q", step] = (codes, scales)
+
+        def project(step, a):
+            band = steps[step][a] // ROWS
+            codes, scales = t["drive_k_q", step]
+            bank = psum.tile([P, M], F32, name="amp")
+            for g in range(SRC_PASSES):
+                cols = slice((a * SRC_PASSES + g) * P, (a * SRC_PASSES + g + 1) * P)
+                nc.tensor.matmul_mx(
+                    out=bank[:],
+                    lhsT=codes[:, cols].bitcast(FP8X4),
+                    lhsT_scale=scales[:, cols],
+                    rhs=src_codes[band * SRC_PASSES + g].bitcast(FP4X4),
+                    rhs_scale=src_planes[band * SRC_PASSES + g],
+                    start=(g == 0),
+                    stop=(g == SRC_PASSES - 1),
+                )
+            t["amp", step, a] = bank
+
+        def loss(i):
+            band, row = divmod(i, ROWS)
+            tile = work.tile([P, M], F32, name="loss", bufs=8)
+            nc.scalar.activation(
+                out=tile[:].rearrange("p (u c e) -> p u c e", u=2, e=2),
+                in_=decay_rows[band].rearrange("p (c u e) -> p u c e", u=2, e=2),
+                func=EXP,
+                scale=dist_f32[:, row : row + 1],
+            )
+            t["loss", i] = tile
+
+        def attenuate(step, a):
+            if a == 0:
+                t["far", step] = work.tile([P, len(steps[step]) * M], BF16, name="far")
+            nc.vector.tensor_tensor(
+                out=t["far", step][:, a * M : (a + 1) * M].rearrange("p (u c e) -> p u c e", u=2, e=2),
+                in0=t["amp", step, a][:].rearrange("p (c u e) -> p u c e", u=2, e=2),
+                in1=t["loss", steps[step][a]][:].rearrange("p (u c e) -> p u c e", u=2, e=2),
+                op=MULT,
+            )
+
+        def turn_far(step):
+            chunks = 2 * len(steps[step])
+            bank = psum.tile([P, chunks, P], F32, name="turned_far", bufs=1)
+            words = t["far", step][:].bitcast(F32)
+            for c in range(chunks):
+                nc.tensor.transpose(bank[:, c, :], words[:, c * P : (c + 1) * P], ident[:])
+            t["turned_far", step] = bank
+
+        def group_far(step, engine):
+            count = len(steps[step])
+            t["far_k", step] = work.tile([P, count * M], BF16, name="far_k", align_bytes=64)
+            copy(
+                engine,
+                t["far_k", step][:].bitcast(F32).rearrange("p (a r u) -> p a r u", a=count, u=2),
+                t["turned_far", step][:].rearrange("p (a u) r -> p a r u", u=2),
+            )
+
+        def receive(step, a):
+            band = steps[step][a] // ROWS
+            codes, scales = t["far_k_q", step]
+            bank = psum.tile([P, Z], F32, name="field")
+            cols = slice(a * P, (a + 1) * P)
+            nc.tensor.matmul_mx(
+                out=bank[:],
+                lhsT=codes[:, cols].bitcast(FP8X4),
+                lhsT_scale=scales[:, cols],
+                rhs=rcv_codes[band].bitcast(FP4X4),
+                rhs_scale=rcv_plane[:, band, :],
+                start=True,
+                stop=True,
+            )
+            t["field", step, a] = bank
+
+        def empty_field(step, a, engine):
+            if a == 0:
+                t["result", step] = work.tile([P, len(steps[step]) * Z], F32, name="result", bufs=6)
+            copy(engine, t["result", step][:, a * Z : (a + 1) * Z], t["field", step, a][:])
+
+        def store(step):
+            band, row = divmod(steps[step][0], ROWS)
+            nc.sync.dma_start(
+                out=fields[band, :, row : row + len(steps[step]), :].rearrange("p j z -> p (j z)"),
+                in_=t["result", step][:],
+            )
+
+        def members(step):
+            return range(len(steps[step])) if 0 <= step < len(steps) else range(0)
+
+        def live(step):
+            return 0 <= step < len(steps)
+
+        last = len(steps) - 1
+        for step in range(LOSS_LEAD):
+            for i in steps[step]:
+                loss(i)
+        for k in range(-DRIVE_LEAD, last + 4):
+            ahead = k + DRIVE_LEAD
+            draining = k + LOSS_LEAD > last
+            for a in members(ahead):
+                turn_drive(steps[ahead][a])
+            if live(k - 1):
+                turn_far(k - 1)
+            if live(k):
+                quantize("drive_k", k, D)
+            for a in members(k - 3):
+                to_scalar = a == 0 and (draining or k % SCALAR_EXTRA == 0)
+                empty_field(k - 3, a, "s" if to_scalar else "v")
+            if live(k - 3):
+                store(k - 3)
+            for a in members(ahead):
+                group_drive(ahead, a, "v" if ahead < VECTOR_HEAD else "s")
+            if live(k - 2):
+                quantize("far_k", k - 2, M)
+            if live(k - 1):
+                group_far(k - 1, "s")
+            for a in members(k):
+                project(k, a)
+            for a in members(k - 2):
+                receive(k - 2, a)
+            if k >= 0:
+                for a in members(k + LOSS_LEAD):
+                    loss(steps[k + LOSS_LEAD][a])
+            for a in members(k):
+                attenuate(k, a)

@@ -27,7 +27,7 @@ SINGLES_TAIL = 2
 SCALAR_EXTRA = 3
 LOSS_LEAD = 2
 DRIVE_LEAD = 1
-VECTOR_HEAD = 2
+VECTOR_HEAD = 3
 
 
 def tile_normal_mode_field_s14_kernel(
@@ -87,35 +87,36 @@ def tile_normal_mode_field_s14_kernel(
             )
             return [tile[:, g, :] for g in range(count)]
 
-        def load_decay(first, count):
-            tile = keep.tile([P, count * M], BF16, name="decay%d" % first)
-            nc.sync.dma_start(
-                out=tile[:],
-                in_=decay[first : first + count].rearrange("b m -> (b m)").partition_broadcast(P),
-            )
-            return [tile[:, b * M : (b + 1) * M] for b in range(count)]
-
         load_drive(0)
+        load_drive(1)
         load_scales(first_plane, src_scales[:SRC_PASSES])
         src_codes = load_words(src_words, 0, SRC_PASSES, "src_first")
-        load_drive(1)
+        decay_words = keep.tile([P, B, 2], F32, name="decay_words")
+        nc.sync.dma_start(out=decay_words[:], in_=decay.bitcast(F32).rearrange("b (c u) -> c b u", u=2))
         dist_bf = keep.tile([P, ROWS], BF16, name="dist_bf")
         nc.sync.dma_start(out=dist_bf[:], in_=dist.rearrange("(p j) -> p j", j=ROWS))
-        decay_rows = load_decay(0, 1)
         load_drive(2)
         load_drive(3)
         load_scales(rcv_plane, rcv_scales)
         rcv_codes = load_words(rcv_words, 0, B, "rcv_all")
         load_drive(4)
         load_scales(rest_plane, src_scales[SRC_PASSES:])
-        decay_rows = decay_rows + load_decay(1, B - 1)
         load_drive(5)
         src_codes = src_codes + load_words(src_words, SRC_PASSES, (B - 1) * SRC_PASSES, "src_rest")
         for step in range(6, len(steps)):
             load_drive(step)
 
         dist_f32 = keep.tile([P, ROWS], F32, name="dist_f32")
-        nc.scalar.copy(out=dist_f32[:], in_=dist_bf[:])
+        decay_rows = []
+
+        def spread_decay(first):
+            bank = psum.tile([P, 4, P], F32, name="field")
+            for c in range(4):
+                column = decay_words[:, first + c // 2, c % 2 : c % 2 + 1]
+                nc.tensor.transpose(bank[:, c, :], column.to_broadcast([P, P]), ident[:])
+            rows = keep.tile([P, 2 * M], BF16, name="decay_rows%d" % first)
+            nc.scalar.copy(out=rows[:].bitcast(F32), in_=bank[:].rearrange("p c r -> p (c r)"))
+            decay_rows.extend([rows[:, :M], rows[:, M:]])
 
         t = {}
 
@@ -175,8 +176,8 @@ def tile_normal_mode_field_s14_kernel(
             band, row = divmod(i, ROWS)
             tile = work.tile([P, M], F32, name="loss", bufs=8)
             nc.scalar.activation(
-                out=tile[:].rearrange("p (u c e) -> p u c e", u=2, e=2),
-                in_=decay_rows[band].rearrange("p (c u e) -> p u c e", u=2, e=2),
+                out=tile[:],
+                in_=decay_rows[band],
                 func=EXP,
                 scale=dist_f32[:, row : row + 1],
             )
@@ -227,7 +228,7 @@ def tile_normal_mode_field_s14_kernel(
 
         def empty_field(step, a, engine):
             if a == 0:
-                t["result", step] = work.tile([P, len(steps[step]) * Z], F32, name="result", bufs=6)
+                t["result", step] = work.tile([P, len(steps[step]) * Z], F32, name="result", bufs=10)
             copy(engine, t["result", step][:, a * Z : (a + 1) * Z], t["field", step, a][:])
 
         def store(step):
@@ -244,14 +245,19 @@ def tile_normal_mode_field_s14_kernel(
             return 0 <= step < len(steps)
 
         last = len(steps) - 1
-        for step in range(LOSS_LEAD):
-            for i in steps[step]:
-                loss(i)
         for k in range(-DRIVE_LEAD, last + 4):
             ahead = k + DRIVE_LEAD
             draining = k + LOSS_LEAD > last
             for a in members(ahead):
                 turn_drive(steps[ahead][a])
+            if ahead == 1:
+                spread_decay(0)
+                nc.scalar.copy(out=dist_f32[:], in_=dist_bf[:])
+                for step in range(LOSS_LEAD):
+                    for i in steps[step]:
+                        loss(i)
+            if ahead == 3:
+                spread_decay(2)
             if live(k - 1):
                 turn_far(k - 1)
             if live(k):

@@ -15,6 +15,7 @@ FP8X4 = mybir.dt.float8_e4m3fn_x4
 FP4X4 = mybir.dt.float4_e2m1fn_x4
 EXP = mybir.ActivationFunctionType.Exp
 MULT = mybir.AluOpType.mult
+ADD = mybir.AluOpType.add
 
 P = 128
 K_PASS = 512
@@ -27,7 +28,9 @@ SINGLES_TAIL = 2
 SCALAR_EXTRA = 3
 LOSS_LEAD = 2
 DRIVE_LEAD = 1
-VECTOR_HEAD = 3
+VECTOR_HEAD = 4
+SORT_FROM = 5
+SORT_COUNT = 1
 
 
 def tile_normal_mode_field_s14_kernel(
@@ -120,16 +123,30 @@ def tile_normal_mode_field_s14_kernel(
 
         t = {}
 
+        shared = [keep.tile([P, D], BF16, name="shared%d" % s, align_bytes=64) for s in range(2)]
+
+        def sort_drive(step, a):
+            rows = shared[step % 2]
+            nc.gpsimd.tensor_scalar(
+                out=rows[:].rearrange("p (u c e) -> p u c e", u=2, e=2),
+                in0=drive_rows[steps[step][a]].rearrange("p (c u e) -> p u c e", u=2, e=2),
+                scalar1=1.0,
+                scalar2=0.0,
+                op0=MULT,
+                op1=ADD,
+            )
+            t["sorted", steps[step][a]] = rows[:].bitcast(F32)
+
         def turn_drive(i):
             bank = psum.tile([P, 2 * SRC_PASSES, P], F32, name="turned_drive", bufs=3)
-            words = drive_rows[i].bitcast(F32)
             for g in range(SRC_PASSES):
                 for u in range(2):
-                    nc.tensor.transpose(
-                        bank[:, 2 * g + u, :],
-                        words[:, g * PASS_WORDS + u : (g + 1) * PASS_WORDS : 2],
-                        ident[:],
-                    )
+                    if ("sorted", i) in t:
+                        first = (u * SRC_PASSES + g) * P
+                        words = t["sorted", i][:, first : first + P]
+                    else:
+                        words = drive_rows[i].bitcast(F32)[:, g * PASS_WORDS + u : (g + 1) * PASS_WORDS : 2]
+                    nc.tensor.transpose(bank[:, 2 * g + u, :], words, ident[:])
             t["turned_drive", i] = bank
 
         def copy(engine, out, in_):
@@ -203,10 +220,10 @@ def tile_normal_mode_field_s14_kernel(
 
         def group_far(step, engine):
             count = len(steps[step])
-            t["far_k", step] = work.tile([P, count * M], BF16, name="far_k", align_bytes=64)
+            t["far_k", step] = shared[step % 2][:, : count * M]
             copy(
                 engine,
-                t["far_k", step][:].bitcast(F32).rearrange("p (a r u) -> p a r u", a=count, u=2),
+                t["far_k", step].bitcast(F32).rearrange("p (a r u) -> p a r u", a=count, u=2),
                 t["turned_far", step][:].rearrange("p (a u) r -> p a r u", u=2),
             )
 
@@ -262,6 +279,11 @@ def tile_normal_mode_field_s14_kernel(
                 turn_far(k - 1)
             if live(k):
                 quantize("drive_k", k, D)
+            if live(k - 2):
+                quantize("far_k", k - 2, M)
+            if k + 2 >= SORT_FROM:
+                for a in members(k + 2)[:SORT_COUNT]:
+                    sort_drive(k + 2, a)
             for a in members(k - 3):
                 to_scalar = a == 0 and (draining or k % SCALAR_EXTRA == 0)
                 empty_field(k - 3, a, "s" if to_scalar else "v")
@@ -269,8 +291,6 @@ def tile_normal_mode_field_s14_kernel(
                 store(k - 3)
             for a in members(ahead):
                 group_drive(ahead, a, "v" if ahead < VECTOR_HEAD else "s")
-            if live(k - 2):
-                quantize("far_k", k - 2, M)
             if live(k - 1):
                 group_far(k - 1, "s")
             for a in members(k):

@@ -23,14 +23,19 @@ PASS_WORDS = K_PASS // 2
 SRC_PASSES = D // K_PASS
 ROWS = T // P
 TILES = B * ROWS
-SINGLES_HEAD = 2
+SINGLES_HEAD = 0
 SINGLES_TAIL = 2
 SCALAR_EXTRA = 3
 LOSS_LEAD = 2
 DRIVE_LEAD = 1
-VECTOR_HEAD = 4
+VECTOR_HEAD = 2
+SPREAD_REST = 0
+LAST_AFTER = 9
 SORT_FROM = 5
 SORT_COUNT = 1
+RCV_AFTER = 3
+SECOND_AFTER = 5
+REST_AFTER = 7
 
 
 def tile_normal_mode_field_s14_kernel(
@@ -55,24 +60,28 @@ def tile_normal_mode_field_s14_kernel(
             return plane
 
         first_plane = cleared_plane(SRC_PASSES, "first_plane")
-        rcv_plane = cleared_plane(B, "rcv_plane")
-        rest_plane = cleared_plane((B - 1) * SRC_PASSES, "rest_plane")
+        rcv_first_plane = cleared_plane(1, "rcv_first_plane")
+        second_plane = cleared_plane(SRC_PASSES, "second_plane")
+        rcv_rest_plane = cleared_plane(B - 1, "rcv_rest_plane")
+        rest_plane = cleared_plane((B - 2) * SRC_PASSES, "rest_plane")
+        rcv_planes = [rcv_first_plane[:, 0, :]] + [rcv_rest_plane[:, b, :] for b in range(B - 1)]
         src_planes = [first_plane[:, g, :] for g in range(SRC_PASSES)]
-        src_planes = src_planes + [rest_plane[:, g, :] for g in range((B - 1) * SRC_PASSES)]
+        src_planes = src_planes + [second_plane[:, g, :] for g in range(SRC_PASSES)]
+        src_planes = src_planes + [rest_plane[:, g, :] for g in range((B - 2) * SRC_PASSES)]
 
         shots = drive.rearrange("b (p j) d -> b p j d", j=ROWS)
         fields = out.rearrange("b (p j) z -> b p j z", j=ROWS)
 
         drive_rows = {}
 
-        def load_drive(step):
-            band, row = divmod(steps[step][0], ROWS)
-            count = len(steps[step])
-            rows = keep.tile([P, count * D], BF16, name="drive%d" % step)
+        def load_drive(tiles):
+            band, row = divmod(tiles[0], ROWS)
+            count = len(tiles)
+            rows = keep.tile([P, count * D], BF16, name="drive%d" % tiles[0])
             nc.sync.dma_start(
                 out=rows[:], in_=shots[band, :, row : row + count, :].rearrange("p j d -> p (j d)")
             )
-            for a, i in enumerate(steps[step]):
+            for a, i in enumerate(tiles):
                 drive_rows[i] = rows[:, a * D : (a + 1) * D]
 
         def load_scales(plane, scales):
@@ -90,24 +99,30 @@ def tile_normal_mode_field_s14_kernel(
             )
             return [tile[:, g, :] for g in range(count)]
 
-        load_drive(0)
-        load_drive(1)
-        load_scales(first_plane, src_scales[:SRC_PASSES])
-        src_codes = load_words(src_words, 0, SRC_PASSES, "src_first")
         decay_words = keep.tile([P, B, 2], F32, name="decay_words")
-        nc.sync.dma_start(out=decay_words[:], in_=decay.bitcast(F32).rearrange("b (c u) -> c b u", u=2))
         dist_bf = keep.tile([P, ROWS], BF16, name="dist_bf")
-        nc.sync.dma_start(out=dist_bf[:], in_=dist.rearrange("(p j) -> p j", j=ROWS))
-        load_drive(2)
-        load_drive(3)
-        load_scales(rcv_plane, rcv_scales)
-        rcv_codes = load_words(rcv_words, 0, B, "rcv_all")
-        load_drive(4)
-        load_scales(rest_plane, src_scales[SRC_PASSES:])
-        load_drive(5)
-        src_codes = src_codes + load_words(src_words, SRC_PASSES, (B - 1) * SRC_PASSES, "src_rest")
-        for step in range(6, len(steps)):
-            load_drive(step)
+        nc.scalar.dma_start(out=decay_words[:], in_=decay.bitcast(F32).rearrange("b (c u) -> c b u", u=2))
+        nc.scalar.dma_start(out=dist_bf[:], in_=dist.rearrange("(p j) -> p j", j=ROWS))
+        for step in range(len(steps)):
+            if step == 0:
+                load_drive(steps[0][:1])
+                load_drive(steps[0][1:])
+                load_scales(first_plane, src_scales[:SRC_PASSES])
+                src_codes = load_words(src_words, 0, SRC_PASSES, "src_first")
+            else:
+                load_drive(steps[step])
+            if step == RCV_AFTER:
+                load_scales(rcv_first_plane, rcv_scales[:1])
+                rcv_codes = load_words(rcv_words, 0, 1, "rcv_first")
+            if step == SECOND_AFTER:
+                load_scales(second_plane, src_scales[SRC_PASSES : 2 * SRC_PASSES])
+                src_codes = src_codes + load_words(src_words, SRC_PASSES, SRC_PASSES, "src_second")
+            if step == REST_AFTER:
+                load_scales(rcv_rest_plane, rcv_scales[1:])
+                rcv_codes = rcv_codes + load_words(rcv_words, 1, B - 1, "rcv_rest")
+            if step == LAST_AFTER:
+                load_scales(rest_plane, src_scales[2 * SRC_PASSES :])
+                src_codes = src_codes + load_words(src_words, 2 * SRC_PASSES, (B - 2) * SRC_PASSES, "src_rest")
 
         dist_f32 = keep.tile([P, ROWS], F32, name="dist_f32")
         decay_rows = []
@@ -165,11 +180,17 @@ def tile_normal_mode_field_s14_kernel(
                 t["turned_drive", steps[step][a]][:].rearrange("p (g u) r -> p g r u", u=2),
             )
 
-        def quantize(key, step, depth):
+        def quantize(key, step, depth, calls=1):
             width = depth * len(steps[step]) // 4
             codes = work.tile([P, width], U32, name=key + "_codes", align_bytes=64)
             scales = work.tile([P, width], U8, name=key + "_scales", align_bytes=64)
-            nc.vector.quantize_mx(out=codes[:].bitcast(FP8X4), scales=scales[:], in_=t[key, step][:])
+            part = width // calls
+            for c in range(0, width, part):
+                nc.vector.quantize_mx(
+                    out=codes[:, c : c + part].bitcast(FP8X4),
+                    scales=scales[:, c : c + part],
+                    in_=t[key, step][:, 4 * c : 4 * (c + part)],
+                )
             t[key + "_q", step] = (codes, scales)
 
         def project(step, a):
@@ -237,7 +258,7 @@ def tile_normal_mode_field_s14_kernel(
                 lhsT=codes[:, cols].bitcast(FP8X4),
                 lhsT_scale=scales[:, cols],
                 rhs=rcv_codes[band].bitcast(FP4X4),
-                rhs_scale=rcv_plane[:, band, :],
+                rhs_scale=rcv_planes[band],
                 start=True,
                 stop=True,
             )
@@ -262,43 +283,49 @@ def tile_normal_mode_field_s14_kernel(
             return 0 <= step < len(steps)
 
         last = len(steps) - 1
-        for k in range(-DRIVE_LEAD, last + 4):
-            ahead = k + DRIVE_LEAD
+        for a in members(0):
+            turn_drive(steps[0][a])
+        spread_decay(0)
+        nc.scalar.copy(out=dist_f32[:], in_=dist_bf[:])
+        for step in range(LOSS_LEAD):
+            for i in steps[step]:
+                loss(i)
+        for a in members(0):
+            group_drive(0, a, "v")
+        quantize("drive_k", 0, D, calls=2)
+        for a in members(0):
+            project(0, a)
+            attenuate(0, a)
+        for k in range(last + 4):
             draining = k + LOSS_LEAD > last
-            for a in members(ahead):
-                turn_drive(steps[ahead][a])
-            if ahead == 1:
-                spread_decay(0)
-                nc.scalar.copy(out=dist_f32[:], in_=dist_bf[:])
-                for step in range(LOSS_LEAD):
-                    for i in steps[step]:
-                        loss(i)
-            if ahead == 3:
+            for a in members(k + 1):
+                turn_drive(steps[k + 1][a])
+            if k == SPREAD_REST:
                 spread_decay(2)
             if live(k - 1):
                 turn_far(k - 1)
-            if live(k):
+            if live(k) and k > 0:
                 quantize("drive_k", k, D)
             if live(k - 2):
                 quantize("far_k", k - 2, M)
-            if k + 2 >= SORT_FROM:
-                for a in members(k + 2)[:SORT_COUNT]:
-                    sort_drive(k + 2, a)
+            if k + 2 >= SORT_FROM and live(k + 2):
+                sort_drive(k + 2, 0)
             for a in members(k - 3):
                 to_scalar = a == 0 and (draining or k % SCALAR_EXTRA == 0)
                 empty_field(k - 3, a, "s" if to_scalar else "v")
             if live(k - 3):
                 store(k - 3)
-            for a in members(ahead):
-                group_drive(ahead, a, "v" if ahead < VECTOR_HEAD else "s")
+            for a in members(k + 1):
+                group_drive(k + 1, a, "v" if k + 1 < VECTOR_HEAD else "s")
             if live(k - 1):
                 group_far(k - 1, "s")
-            for a in members(k):
-                project(k, a)
+            if k > 0:
+                for a in members(k):
+                    project(k, a)
             for a in members(k - 2):
                 receive(k - 2, a)
-            if k >= 0:
-                for a in members(k + LOSS_LEAD):
-                    loss(steps[k + LOSS_LEAD][a])
-            for a in members(k):
-                attenuate(k, a)
+            for a in members(k + LOSS_LEAD):
+                loss(steps[k + LOSS_LEAD][a])
+            if k > 0:
+                for a in members(k):
+                    attenuate(k, a)

@@ -15,36 +15,38 @@ FP8X4 = mybir.dt.float8_e4m3fn_x4
 FP4X4 = mybir.dt.float4_e2m1fn_x4
 EXP = mybir.ActivationFunctionType.Exp
 MULT = mybir.AluOpType.mult
-ADD = mybir.AluOpType.add
 
 P = 128
-K_PASS = 512
+PACK = 4
+K_PASS = P * PACK
 PASS_WORDS = K_PASS // 2
 SRC_PASSES = D // K_PASS
 ROWS = T // P
 TILES = B * ROWS
-SINGLES_HEAD = 0
-SINGLES_TAIL = 2
-SCALAR_EXTRA = 3
-LOSS_LEAD = 2
-DRIVE_LEAD = 1
-VECTOR_HEAD = 2
-SPREAD_REST = 0
-LAST_AFTER = 9
-SORT_FROM = 5
-SORT_COUNT = 1
-RCV_AFTER = 3
-SECOND_AFTER = 5
-REST_AFTER = 7
+PAIR = 2
+STEPS_PER_BAND = ROWS // PAIR
+BANK_CHUNKS = 4
+QUADRANT = 32
+SCALE_ROWS = 16
+
+LOSS_LEAD = 5
+VECTOR_TILES = 3
+VECTOR_REORDER_AT = 2
+SRC_SECOND_AFTER = 1
+RCV_FIRST_AFTER = 2
+SRC_REST_AFTER = 4
+RCV_REST_AFTER = 5
+RESULT_BUFS = 10
 
 
 def tile_normal_mode_field_s14_kernel(
     tc, drive, src_words, src_scales, decay, dist, rcv_words, rcv_scales, out
 ):
     nc = tc.nc
-    steps = [[i] for i in range(SINGLES_HEAD)]
-    steps = steps + [[i, i + 1] for i in range(SINGLES_HEAD, TILES - SINGLES_TAIL, 2)]
-    steps = steps + [[i] for i in range(TILES - SINGLES_TAIL, TILES)]
+    steps = [[i, i + 1] for i in range(0, TILES - PAIR, PAIR)] + [[i] for i in range(TILES - PAIR, TILES)]
+    last = len(steps) - 1
+    spans = [(0, PAIR), (PAIR, 2 * PAIR)] + [(i, i + 2 * PAIR) for i in range(2 * PAIR, TILES, 2 * PAIR)]
+
     with ExitStack() as ctx:
         keep = ctx.enter_context(tc.tile_pool(name="keep", bufs=1))
         work = ctx.enter_context(tc.tile_pool(name="work", bufs=3))
@@ -54,24 +56,24 @@ def tile_normal_mode_field_s14_kernel(
         ident = keep.tile([P, P], F32, name="ident")
         make_identity(nc, ident[:])
 
+
         def cleared_plane(passes, name):
             plane = keep.tile([P, passes, M], U8, name=name, align_bytes=64)
             nc.vector.memset(plane[:].bitcast(I32), 0)
             return plane
 
-        first_plane = cleared_plane(SRC_PASSES, "first_plane")
+        src_first_plane = cleared_plane(SRC_PASSES, "src_first_plane")
         rcv_first_plane = cleared_plane(1, "rcv_first_plane")
-        second_plane = cleared_plane(SRC_PASSES, "second_plane")
+        src_second_plane = cleared_plane(SRC_PASSES, "src_second_plane")
         rcv_rest_plane = cleared_plane(B - 1, "rcv_rest_plane")
-        rest_plane = cleared_plane((B - 2) * SRC_PASSES, "rest_plane")
+        src_rest_plane = cleared_plane((B - 2) * SRC_PASSES, "src_rest_plane")
         rcv_planes = [rcv_first_plane[:, 0, :]] + [rcv_rest_plane[:, b, :] for b in range(B - 1)]
-        src_planes = [first_plane[:, g, :] for g in range(SRC_PASSES)]
-        src_planes = src_planes + [second_plane[:, g, :] for g in range(SRC_PASSES)]
-        src_planes = src_planes + [rest_plane[:, g, :] for g in range((B - 2) * SRC_PASSES)]
+        src_raw_planes = [src_first_plane[:], src_second_plane[:]] + [
+            src_rest_plane[:, SRC_PASSES * b : SRC_PASSES * (b + 1), :] for b in range(B - 2)
+        ]
 
         shots = drive.rearrange("b (p j) d -> b p j d", j=ROWS)
         fields = out.rearrange("b (p j) z -> b p j z", j=ROWS)
-
         drive_rows = {}
 
         def load_drive(tiles):
@@ -85,10 +87,10 @@ def tile_normal_mode_field_s14_kernel(
                 drive_rows[i] = rows[:, a * D : (a + 1) * D]
 
         def load_scales(plane, scales):
-            for r in range(4):
+            for r in range(SCALE_ROWS * QUADRANT // P):
                 nc.sync.dma_start(
-                    out=plane[:].bitcast(I32)[r:P:32, :, :],
-                    in_=scales.bitcast(I32)[:, r:16:4, :].rearrange("g q n -> q g n"),
+                    out=plane[:].bitcast(I32)[r:P:QUADRANT, :, :],
+                    in_=scales.bitcast(I32)[:, r:SCALE_ROWS:4, :].rearrange("g q n -> q g n"),
                 )
 
         def load_words(words, first, count, name):
@@ -97,160 +99,173 @@ def tile_normal_mode_field_s14_kernel(
                 out=tile[:].bitcast(I32),
                 in_=words.bitcast(I32)[first : first + count].rearrange("g p n -> p g n"),
             )
-            return [tile[:, g, :] for g in range(count)]
+            return tile
 
-        decay_words = keep.tile([P, B, 2], F32, name="decay_words")
         dist_bf = keep.tile([P, ROWS], BF16, name="dist_bf")
-        nc.scalar.dma_start(out=decay_words[:], in_=decay.bitcast(F32).rearrange("b (c u) -> c b u", u=2))
+        decay_bf = keep.tile([P, B, PACK], BF16, name="decay_bf")
         nc.scalar.dma_start(out=dist_bf[:], in_=dist.rearrange("(p j) -> p j", j=ROWS))
-        for step in range(len(steps)):
-            if step == 0:
-                load_drive(steps[0][:1])
-                load_drive(steps[0][1:])
-                load_scales(first_plane, src_scales[:SRC_PASSES])
-                src_codes = load_words(src_words, 0, SRC_PASSES, "src_first")
-            else:
-                load_drive(steps[step])
-            if step == RCV_AFTER:
+        nc.scalar.dma_start(out=decay_bf[:], in_=decay.rearrange("b (p t) -> p b t", t=PACK))
+
+        src_raw_codes = {0: load_words(src_words, 0, SRC_PASSES, "src_first")[:]}
+        load_drive(steps[0][:1])
+        load_scales(src_first_plane, src_scales[:SRC_PASSES])
+        load_drive(steps[0][1:])
+        rcv_codes = {}
+        for step in range(1, len(steps)):
+            load_drive(steps[step])
+            if step == SRC_SECOND_AFTER:
+                src_raw_codes[1] = load_words(src_words, SRC_PASSES, SRC_PASSES, "src_second")[:]
+            if step == RCV_FIRST_AFTER:
                 load_scales(rcv_first_plane, rcv_scales[:1])
-                rcv_codes = load_words(rcv_words, 0, 1, "rcv_first")
-            if step == SECOND_AFTER:
-                load_scales(second_plane, src_scales[SRC_PASSES : 2 * SRC_PASSES])
-                src_codes = src_codes + load_words(src_words, SRC_PASSES, SRC_PASSES, "src_second")
-            if step == REST_AFTER:
+                rcv_codes[0] = load_words(rcv_words, 0, 1, "rcv_first")[:, 0, :]
+            if step == RCV_FIRST_AFTER + 1:
+                load_scales(src_second_plane, src_scales[SRC_PASSES : 2 * SRC_PASSES])
+            if step == SRC_REST_AFTER:
+                src_rest = load_words(src_words, 2 * SRC_PASSES, (B - 2) * SRC_PASSES, "src_rest")
+                for b in range(2, B):
+                    src_raw_codes[b] = src_rest[:, SRC_PASSES * (b - 2) : SRC_PASSES * (b - 1), :]
+            if step == RCV_REST_AFTER:
                 load_scales(rcv_rest_plane, rcv_scales[1:])
-                rcv_codes = rcv_codes + load_words(rcv_words, 1, B - 1, "rcv_rest")
-            if step == LAST_AFTER:
-                load_scales(rest_plane, src_scales[2 * SRC_PASSES :])
-                src_codes = src_codes + load_words(src_words, 2 * SRC_PASSES, (B - 2) * SRC_PASSES, "src_rest")
+                rcv_rest = load_words(rcv_words, 1, B - 1, "rcv_rest")
+                for b in range(1, B):
+                    rcv_codes[b] = rcv_rest[:, b - 1, :]
+            if step == RCV_REST_AFTER + 1:
+                load_scales(src_rest_plane, src_scales[2 * SRC_PASSES :])
 
+
+        made = {}
         dist_f32 = keep.tile([P, ROWS], F32, name="dist_f32")
-        decay_rows = []
+        decay_f32 = keep.tile([P, B, PACK], F32, name="decay_f32")
+        dist_rows = keep.tile([P, T], F32, name="dist_rows")
 
-        def spread_decay(first):
-            bank = psum.tile([P, 4, P], F32, name="field")
-            for c in range(4):
-                column = decay_words[:, first + c // 2, c % 2 : c % 2 + 1]
+        def spread_dist(first):
+            bank = psum.tile([P, BANK_CHUNKS, P], F32, name="field")
+            for c in range(BANK_CHUNKS):
+                column = dist_f32[:, first + c : first + c + 1]
                 nc.tensor.transpose(bank[:, c, :], column.to_broadcast([P, P]), ident[:])
-            rows = keep.tile([P, 2 * M], BF16, name="decay_rows%d" % first)
-            nc.scalar.copy(out=rows[:].bitcast(F32), in_=bank[:].rearrange("p c r -> p (c r)"))
-            decay_rows.extend([rows[:, :M], rows[:, M:]])
-
-        t = {}
-
-        shared = [keep.tile([P, D], BF16, name="shared%d" % s, align_bytes=64) for s in range(2)]
-
-        def sort_drive(step, a):
-            rows = shared[step % 2]
-            nc.gpsimd.tensor_scalar(
-                out=rows[:].rearrange("p (u c e) -> p u c e", u=2, e=2),
-                in0=drive_rows[steps[step][a]].rearrange("p (c u e) -> p u c e", u=2, e=2),
-                scalar1=1.0,
-                scalar2=0.0,
-                op0=MULT,
-                op1=ADD,
+            nc.scalar.copy(
+                out=dist_rows[:, first * P : (first + BANK_CHUNKS) * P],
+                in_=bank[:].rearrange("p c r -> p (c r)"),
             )
-            t["sorted", steps[step][a]] = rows[:].bitcast(F32)
+
+        def order_codes(band, slot, engine, tag):
+            codes = keep.tile([P, SRC_PASSES, 2 * P], U8, name="src_codes", tag=tag, align_bytes=64)
+            engine.tensor_copy(
+                out=codes[:].rearrange("p g (c e) -> p g c e", e=2),
+                in_=src_raw_codes[band].rearrange("p g (c t e) -> p g c t e", t=PACK, e=2)[:, :, :, slot, :],
+            )
+            made["src_codes", band, slot] = codes
+
+        def order_scales(band):
+            plane = keep.tile([P, SRC_PASSES, PACK, P], U8, name="src_plane%d" % band, align_bytes=64)
+            nc.vector.tensor_copy(
+                out=plane[:], in_=src_raw_planes[band].rearrange("p g (c t) -> p g t c", t=PACK)
+            )
+            made["src_plane", band] = plane
+
+        def gpsimd_job(k):
+            band, slot = divmod(k, STEPS_PER_BAND)
+            return (band + 1, slot) if slot > 0 and band + 1 < B else None
 
         def turn_drive(i):
             bank = psum.tile([P, 2 * SRC_PASSES, P], F32, name="turned_drive", bufs=3)
+            words = drive_rows[i].bitcast(F32)
             for g in range(SRC_PASSES):
                 for u in range(2):
-                    if ("sorted", i) in t:
-                        first = (u * SRC_PASSES + g) * P
-                        words = t["sorted", i][:, first : first + P]
-                    else:
-                        words = drive_rows[i].bitcast(F32)[:, g * PASS_WORDS + u : (g + 1) * PASS_WORDS : 2]
-                    nc.tensor.transpose(bank[:, 2 * g + u, :], words, ident[:])
-            t["turned_drive", i] = bank
+                    nc.tensor.transpose(
+                        bank[:, 2 * g + u, :],
+                        words[:, g * PASS_WORDS + u : (g + 1) * PASS_WORDS : 2],
+                        ident[:],
+                    )
+            made["turned_drive", i] = bank
 
-        def copy(engine, out, in_):
-            if engine == "v":
-                nc.vector.tensor_copy(out=out, in_=in_)
+        def copy_out(on_vector, target, source):
+            if on_vector:
+                nc.vector.tensor_copy(out=target, in_=source)
             else:
-                nc.scalar.copy(out=out, in_=in_)
+                nc.scalar.copy(out=target, in_=source)
 
-        def group_drive(step, a, engine):
+        def group_drive(step, a):
             if a == 0:
-                t["drive_k", step] = work.tile([P, len(steps[step]) * D], BF16, name="drive_k", align_bytes=64, bufs=4)
-            words = t["drive_k", step][:].bitcast(F32)[:, a * D // 2 : (a + 1) * D // 2]
-            copy(
-                engine,
+                made["drive_k", step] = work.tile(
+                    [P, len(steps[step]) * D], BF16, name="drive_k", align_bytes=64
+                )
+            words = made["drive_k", step][:].bitcast(F32)[:, a * D // 2 : (a + 1) * D // 2]
+            copy_out(
+                steps[step][a] < VECTOR_TILES,
                 words.rearrange("p (g r u) -> p g r u", g=SRC_PASSES, u=2),
-                t["turned_drive", steps[step][a]][:].rearrange("p (g u) r -> p g r u", u=2),
+                made["turned_drive", steps[step][a]][:].rearrange("p (g u) r -> p g r u", u=2),
             )
 
-        def quantize(key, step, depth, calls=1):
-            width = depth * len(steps[step]) // 4
-            codes = work.tile([P, width], U32, name=key + "_codes", align_bytes=64)
-            scales = work.tile([P, width], U8, name=key + "_scales", align_bytes=64)
-            part = width // calls
-            for c in range(0, width, part):
-                nc.vector.quantize_mx(
-                    out=codes[:, c : c + part].bitcast(FP8X4),
-                    scales=scales[:, c : c + part],
-                    in_=t[key, step][:, 4 * c : 4 * (c + part)],
+        def quantize(key, step, depth, tiles):
+            if tiles[0] == 0:
+                width = depth * len(steps[step]) // PACK
+                made[key + "_q", step] = (
+                    work.tile([P, width], U32, name=key + "_codes", align_bytes=64),
+                    work.tile([P, width], U8, name=key + "_scales", align_bytes=64),
                 )
-            t[key + "_q", step] = (codes, scales)
+            codes, scales = made[key + "_q", step]
+            first, end = tiles[0] * depth // PACK, (tiles[-1] + 1) * depth // PACK
+            nc.vector.quantize_mx(
+                out=codes[:, first:end].bitcast(FP8X4),
+                scales=scales[:, first:end],
+                in_=made[key, step][:, PACK * first : PACK * end],
+            )
 
         def project(step, a):
             band = steps[step][a] // ROWS
-            codes, scales = t["drive_k_q", step]
-            bank = psum.tile([P, M], F32, name="amp")
-            for g in range(SRC_PASSES):
-                cols = slice((a * SRC_PASSES + g) * P, (a * SRC_PASSES + g + 1) * P)
-                nc.tensor.matmul_mx(
-                    out=bank[:],
-                    lhsT=codes[:, cols].bitcast(FP8X4),
-                    lhsT_scale=scales[:, cols],
-                    rhs=src_codes[band * SRC_PASSES + g].bitcast(FP4X4),
-                    rhs_scale=src_planes[band * SRC_PASSES + g],
-                    start=(g == 0),
-                    stop=(g == SRC_PASSES - 1),
-                )
-            t["amp", step, a] = bank
+            codes, scales = made["drive_k_q", step]
+            bank = psum.tile([P, PACK, P], F32, name="amp", bufs=3)
+            for slot in range(PACK):
+                for g in range(SRC_PASSES):
+                    cols = slice((a * SRC_PASSES + g) * P, (a * SRC_PASSES + g + 1) * P)
+                    nc.tensor.matmul_mx(
+                        out=bank[:, slot, :],
+                        lhsT=made["src_codes", band, slot][:, g, :].bitcast(FP4X4),
+                        lhsT_scale=made["src_plane", band][:, g, slot, :],
+                        rhs=codes[:, cols].bitcast(FP8X4),
+                        rhs_scale=scales[:, cols],
+                        start=(g == 0),
+                        stop=(g == SRC_PASSES - 1),
+                    )
+            made["amp", step, a] = bank
 
-        def loss(i):
-            band, row = divmod(i, ROWS)
-            tile = work.tile([P, M], F32, name="loss", bufs=8)
-            nc.scalar.activation(
-                out=tile[:],
-                in_=decay_rows[band],
-                func=EXP,
-                scale=dist_f32[:, row : row + 1],
-            )
-            t["loss", i] = tile
+        loss_jobs = [(first, end, slot) for first, end in spans for slot in range(PACK)]
+
+        def losses_until(tiles):
+            while loss_jobs and loss_jobs[0][0] + (loss_jobs[0][1] - loss_jobs[0][0]) * loss_jobs[0][2] / PACK < tiles:
+                first, end, slot = loss_jobs.pop(0)
+                band, row = divmod(first, ROWS)
+                if slot == 0:
+                    made["loss", first] = work.tile([P, PACK, (end - first) * P], F32, name="loss")
+                nc.scalar.activation(
+                    out=made["loss", first][:, slot, :],
+                    in_=dist_rows[:, row * P : (row + end - first) * P],
+                    func=EXP,
+                    scale=decay_f32[:, band, slot : slot + 1],
+                )
+                if slot == PACK - 1:
+                    for i in range(first, end):
+                        made["tile_loss", i] = made["loss", first][:, :, (i - first) * P : (i - first + 1) * P]
 
         def attenuate(step, a):
             if a == 0:
-                t["far", step] = work.tile([P, len(steps[step]) * M], BF16, name="far")
+                shape = [P, len(steps[step]) * M]
+                if gpsimd_job(step + 1):
+                    far = keep.tile(shape, BF16, name="far_k", tag="far%d" % step, align_bytes=64)
+                else:
+                    far = work.tile(shape, BF16, name="far_k", align_bytes=64)
+                made["far_k", step] = far
             nc.vector.tensor_tensor(
-                out=t["far", step][:, a * M : (a + 1) * M].rearrange("p (u c e) -> p u c e", u=2, e=2),
-                in0=t["amp", step, a][:].rearrange("p (c u e) -> p u c e", u=2, e=2),
-                in1=t["loss", steps[step][a]][:].rearrange("p (u c e) -> p u c e", u=2, e=2),
+                out=made["far_k", step][:, a * M : (a + 1) * M].rearrange("p (c i t) -> p c t i", i=2, t=PACK),
+                in0=made["tile_loss", steps[step][a]].rearrange("p t (c i) -> p c t i", i=2),
+                in1=made["amp", step, a][:].rearrange("p t (c i) -> p c t i", i=2),
                 op=MULT,
-            )
-
-        def turn_far(step):
-            chunks = 2 * len(steps[step])
-            bank = psum.tile([P, chunks, P], F32, name="turned_far", bufs=1)
-            words = t["far", step][:].bitcast(F32)
-            for c in range(chunks):
-                nc.tensor.transpose(bank[:, c, :], words[:, c * P : (c + 1) * P], ident[:])
-            t["turned_far", step] = bank
-
-        def group_far(step, engine):
-            count = len(steps[step])
-            t["far_k", step] = shared[step % 2][:, : count * M]
-            copy(
-                engine,
-                t["far_k", step].bitcast(F32).rearrange("p (a r u) -> p a r u", a=count, u=2),
-                t["turned_far", step][:].rearrange("p (a u) r -> p a r u", u=2),
             )
 
         def receive(step, a):
             band = steps[step][a] // ROWS
-            codes, scales = t["far_k_q", step]
+            codes, scales = made["far_k_q", step]
             bank = psum.tile([P, Z], F32, name="field")
             cols = slice(a * P, (a + 1) * P)
             nc.tensor.matmul_mx(
@@ -262,70 +277,84 @@ def tile_normal_mode_field_s14_kernel(
                 start=True,
                 stop=True,
             )
-            t["field", step, a] = bank
+            made["field", step, a] = bank
 
-        def empty_field(step, a, engine):
+        def empty_field(step, a):
             if a == 0:
-                t["result", step] = work.tile([P, len(steps[step]) * Z], F32, name="result", bufs=10)
-            copy(engine, t["result", step][:, a * Z : (a + 1) * Z], t["field", step, a][:])
+                made["result", step] = work.tile(
+                    [P, len(steps[step]) * Z], F32, name="result", bufs=RESULT_BUFS
+                )
+            copy_out(
+                a > 0 and len(loss_jobs) > 0,
+                made["result", step][:, a * Z : (a + 1) * Z],
+                made["field", step, a][:],
+            )
 
         def store(step):
             band, row = divmod(steps[step][0], ROWS)
             nc.sync.dma_start(
                 out=fields[band, :, row : row + len(steps[step]), :].rearrange("p j z -> p (j z)"),
-                in_=t["result", step][:],
+                in_=made["result", step][:],
             )
 
         def members(step):
-            return range(len(steps[step])) if 0 <= step < len(steps) else range(0)
+            return range(len(steps[step])) if 0 <= step <= last else range(0)
 
-        def live(step):
-            return 0 <= step < len(steps)
 
-        last = len(steps) - 1
-        for a in members(0):
-            turn_drive(steps[0][a])
-        spread_decay(0)
         nc.scalar.copy(out=dist_f32[:], in_=dist_bf[:])
-        for step in range(LOSS_LEAD):
-            for i in steps[step]:
-                loss(i)
+        spread_dist(0)
+        nc.scalar.copy(out=decay_f32[:], in_=decay_bf[:])
+        losses_until(PAIR)
+        for slot in range(PACK):
+            order_codes(0, slot, nc.vector, "first%d" % slot)
+        turn_drive(steps[0][0])
+        group_drive(0, 0)
+        order_scales(0)
+        quantize("drive_k", 0, D, [0])
+        turn_drive(steps[0][1])
+        spread_dist(BANK_CHUNKS)
+        group_drive(0, 1)
+        project(0, 0)
+        quantize("drive_k", 0, D, [1])
+        for i in steps[1]:
+            turn_drive(i)
+        project(0, 1)
+        losses_until(2 * PAIR)
         for a in members(0):
-            group_drive(0, a, "v")
-        quantize("drive_k", 0, D, calls=2)
-        for a in members(0):
-            project(0, a)
             attenuate(0, a)
-        for k in range(last + 4):
-            draining = k + LOSS_LEAD > last
-            for a in members(k + 1):
-                turn_drive(steps[k + 1][a])
-            if k == SPREAD_REST:
-                spread_decay(2)
-            if live(k - 1):
-                turn_far(k - 1)
-            if live(k) and k > 0:
-                quantize("drive_k", k, D)
-            if live(k - 2):
-                quantize("far_k", k - 2, M)
-            if k + 2 >= SORT_FROM and live(k + 2):
-                sort_drive(k + 2, 0)
-            for a in members(k - 3):
-                to_scalar = a == 0 and (draining or k % SCALAR_EXTRA == 0)
-                empty_field(k - 3, a, "s" if to_scalar else "v")
-            if live(k - 3):
-                store(k - 3)
-            for a in members(k + 1):
-                group_drive(k + 1, a, "v" if k + 1 < VECTOR_HEAD else "s")
-            if live(k - 1):
-                group_far(k - 1, "s")
-            if k > 0:
-                for a in members(k):
-                    project(k, a)
+            group_drive(1, a)
+        for i in steps[2]:
+            turn_drive(i)
+        group_drive(2, 0)
+        quantize("drive_k", 1, D, members(1))
+        group_drive(2, 1)
+        losses_until(LOSS_LEAD)
+
+
+        for k in range(1, last + 3):
+            for a in members(k + 2):
+                turn_drive(steps[k + 2][a])
+            if members(k + 1):
+                quantize("drive_k", k + 1, D, members(k + 1))
+            if members(k - 1):
+                quantize("far_k", k - 1, M, members(k - 1))
+            job = gpsimd_job(k)
+            if job:
+                order_codes(job[0], job[1], nc.gpsimd, "far%d" % (k - 1))
             for a in members(k - 2):
-                receive(k - 2, a)
-            for a in members(k + LOSS_LEAD):
-                loss(steps[k + LOSS_LEAD][a])
-            if k > 0:
-                for a in members(k):
-                    attenuate(k, a)
+                empty_field(k - 2, a)
+            if members(k - 2):
+                store(k - 2)
+            for a in members(k + 2):
+                group_drive(k + 2, a)
+            for a in members(k):
+                project(k, a)
+            for a in members(k - 1):
+                receive(k - 1, a)
+            if members(k):
+                losses_until(steps[k][-1] + LOSS_LEAD)
+            for a in members(k):
+                attenuate(k, a)
+            if job and job[1] == VECTOR_REORDER_AT:
+                order_codes(job[0], 0, nc.vector, "slot0_%d" % job[0])
+                order_scales(job[0])

from contextlib import ExitStack

import concourse.mybir as mybir
from concourse.masks import make_identity

B, T, D, M, Z = 4, 1024, 1024, 512, 512
FLOPS = 2 * B * T * (D * M + M * Z)

F32 = mybir.dt.float32
BF16 = mybir.dt.bfloat16
I32 = mybir.dt.int32
U32 = mybir.dt.uint32
U8 = mybir.dt.uint8
FP8X4 = mybir.dt.float8_e4m3fn_x4
FP4X4 = mybir.dt.float4_e2m1fn_x4
EXP = mybir.ActivationFunctionType.Exp
MULT = mybir.AluOpType.mult

P = 128
PACK = 4
K_PASS = P * PACK
PASS_WORDS = K_PASS // 2
SRC_PASSES = D // K_PASS
ROWS = T // P
TILES = B * ROWS
PAIR = 2
STEPS_PER_BAND = ROWS // PAIR
BANK_CHUNKS = 4
QUADRANT = 32
SCALE_ROWS = 16

LOSS_LEAD = 5
VECTOR_TILES = 3
VECTOR_REORDER_AT = 2
SRC_SECOND_AFTER = 1
RCV_FIRST_AFTER = 2
SRC_REST_AFTER = 4
RCV_REST_AFTER = 5
RESULT_BUFS = 10


def tile_normal_mode_field_s14_kernel(
    tc, drive, src_words, src_scales, decay, dist, rcv_words, rcv_scales, out
):
    nc = tc.nc
    steps = [[i, i + 1] for i in range(0, TILES - PAIR, PAIR)] + [[i] for i in range(TILES - PAIR, TILES)]
    last = len(steps) - 1
    spans = [(0, PAIR), (PAIR, 2 * PAIR)] + [(i, i + 2 * PAIR) for i in range(2 * PAIR, TILES, 2 * PAIR)]

    with ExitStack() as ctx:
        keep = ctx.enter_context(tc.tile_pool(name="keep", bufs=1))
        work = ctx.enter_context(tc.tile_pool(name="work", bufs=3))
        psum = ctx.enter_context(tc.psum_pool(name="psum", bufs=2))
        ctx.enter_context(tc.manual_schedule())

        ident = keep.tile([P, P], F32, name="ident")
        make_identity(nc, ident[:])


        def cleared_plane(passes, name):
            plane = keep.tile([P, passes, M], U8, name=name, align_bytes=64)
            nc.vector.memset(plane[:].bitcast(I32), 0)
            return plane

        src_first_plane = cleared_plane(SRC_PASSES, "src_first_plane")
        rcv_first_plane = cleared_plane(1, "rcv_first_plane")
        src_second_plane = cleared_plane(SRC_PASSES, "src_second_plane")
        rcv_rest_plane = cleared_plane(B - 1, "rcv_rest_plane")
        src_rest_plane = cleared_plane((B - 2) * SRC_PASSES, "src_rest_plane")
        rcv_planes = [rcv_first_plane[:, 0, :]] + [rcv_rest_plane[:, b, :] for b in range(B - 1)]
        src_raw_planes = [src_first_plane[:], src_second_plane[:]] + [
            src_rest_plane[:, SRC_PASSES * b : SRC_PASSES * (b + 1), :] for b in range(B - 2)
        ]

        shots = drive.rearrange("b (p j) d -> b p j d", j=ROWS)
        fields = out.rearrange("b (p j) z -> b p j z", j=ROWS)
        drive_rows = {}

        def load_drive(tiles):
            band, row = divmod(tiles[0], ROWS)
            count = len(tiles)
            rows = keep.tile([P, count * D], BF16, name="drive%d" % tiles[0])
            nc.sync.dma_start(
                out=rows[:], in_=shots[band, :, row : row + count, :].rearrange("p j d -> p (j d)")
            )
            for a, i in enumerate(tiles):
                drive_rows[i] = rows[:, a * D : (a + 1) * D]

        def load_scales(plane, scales):
            for r in range(SCALE_ROWS * QUADRANT // P):
                nc.sync.dma_start(
                    out=plane[:].bitcast(I32)[r:P:QUADRANT, :, :],
                    in_=scales.bitcast(I32)[:, r:SCALE_ROWS:4, :].rearrange("g q n -> q g n"),
                )

        def load_words(words, first, count, name):
            tile = keep.tile([P, count, 2 * M], U8, name=name, align_bytes=64)
            nc.sync.dma_start(
                out=tile[:].bitcast(I32),
                in_=words.bitcast(I32)[first : first + count].rearrange("g p n -> p g n"),
            )
            return tile

        dist_bf = keep.tile([P, ROWS], BF16, name="dist_bf")
        decay_bf = keep.tile([P, B, PACK], BF16, name="decay_bf")
        nc.scalar.dma_start(out=dist_bf[:], in_=dist.rearrange("(p j) -> p j", j=ROWS))
        nc.scalar.dma_start(out=decay_bf[:], in_=decay.rearrange("b (p t) -> p b t", t=PACK))

        src_raw_codes = {0: load_words(src_words, 0, SRC_PASSES, "src_first")[:]}
        load_drive(steps[0][:1])
        load_scales(src_first_plane, src_scales[:SRC_PASSES])
        load_drive(steps[0][1:])
        rcv_codes = {}
        for step in range(1, len(steps)):
            load_drive(steps[step])
            if step == SRC_SECOND_AFTER:
                src_raw_codes[1] = load_words(src_words, SRC_PASSES, SRC_PASSES, "src_second")[:]
            if step == RCV_FIRST_AFTER:
                load_scales(rcv_first_plane, rcv_scales[:1])
                rcv_codes[0] = load_words(rcv_words, 0, 1, "rcv_first")[:, 0, :]
            if step == RCV_FIRST_AFTER + 1:
                load_scales(src_second_plane, src_scales[SRC_PASSES : 2 * SRC_PASSES])
            if step == SRC_REST_AFTER:
                src_rest = load_words(src_words, 2 * SRC_PASSES, (B - 2) * SRC_PASSES, "src_rest")
                for b in range(2, B):
                    src_raw_codes[b] = src_rest[:, SRC_PASSES * (b - 2) : SRC_PASSES * (b - 1), :]
            if step == RCV_REST_AFTER:
                load_scales(rcv_rest_plane, rcv_scales[1:])
                rcv_rest = load_words(rcv_words, 1, B - 1, "rcv_rest")
                for b in range(1, B):
                    rcv_codes[b] = rcv_rest[:, b - 1, :]
            if step == RCV_REST_AFTER + 1:
                load_scales(src_rest_plane, src_scales[2 * SRC_PASSES :])


        made = {}
        dist_f32 = keep.tile([P, ROWS], F32, name="dist_f32")
        decay_f32 = keep.tile([P, B, PACK], F32, name="decay_f32")
        dist_rows = keep.tile([P, T], F32, name="dist_rows")

        def spread_dist(first):
            bank = psum.tile([P, BANK_CHUNKS, P], F32, name="field")
            for c in range(BANK_CHUNKS):
                column = dist_f32[:, first + c : first + c + 1]
                nc.tensor.transpose(bank[:, c, :], column.to_broadcast([P, P]), ident[:])
            nc.scalar.copy(
                out=dist_rows[:, first * P : (first + BANK_CHUNKS) * P],
                in_=bank[:].rearrange("p c r -> p (c r)"),
            )

        def order_codes(band, slot, engine, tag):
            codes = keep.tile([P, SRC_PASSES, 2 * P], U8, name="src_codes", tag=tag, align_bytes=64)
            engine.tensor_copy(
                out=codes[:].rearrange("p g (c e) -> p g c e", e=2),
                in_=src_raw_codes[band].rearrange("p g (c t e) -> p g c t e", t=PACK, e=2)[:, :, :, slot, :],
            )
            made["src_codes", band, slot] = codes

        def order_scales(band):
            plane = keep.tile([P, SRC_PASSES, PACK, P], U8, name="src_plane%d" % band, align_bytes=64)
            nc.vector.tensor_copy(
                out=plane[:], in_=src_raw_planes[band].rearrange("p g (c t) -> p g t c", t=PACK)
            )
            made["src_plane", band] = plane

        def gpsimd_job(k):
            band, slot = divmod(k, STEPS_PER_BAND)
            return (band + 1, slot) if slot > 0 and band + 1 < B else None

        def turn_drive(i):
            bank = psum.tile([P, 2 * SRC_PASSES, P], F32, name="turned_drive", bufs=3)
            words = drive_rows[i].bitcast(F32)
            for g in range(SRC_PASSES):
                for u in range(2):
                    nc.tensor.transpose(
                        bank[:, 2 * g + u, :],
                        words[:, g * PASS_WORDS + u : (g + 1) * PASS_WORDS : 2],
                        ident[:],
                    )
            made["turned_drive", i] = bank

        def copy_out(on_vector, target, source):
            if on_vector:
                nc.vector.tensor_copy(out=target, in_=source)
            else:
                nc.scalar.copy(out=target, in_=source)

        def group_drive(step, a):
            if a == 0:
                made["drive_k", step] = work.tile(
                    [P, len(steps[step]) * D], BF16, name="drive_k", align_bytes=64
                )
            words = made["drive_k", step][:].bitcast(F32)[:, a * D // 2 : (a + 1) * D // 2]
            copy_out(
                steps[step][a] < VECTOR_TILES,
                words.rearrange("p (g r u) -> p g r u", g=SRC_PASSES, u=2),
                made["turned_drive", steps[step][a]][:].rearrange("p (g u) r -> p g r u", u=2),
            )

        def quantize(key, step, depth, tiles):
            if tiles[0] == 0:
                width = depth * len(steps[step]) // PACK
                made[key + "_q", step] = (
                    work.tile([P, width], U32, name=key + "_codes", align_bytes=64),
                    work.tile([P, width], U8, name=key + "_scales", align_bytes=64),
                )
            codes, scales = made[key + "_q", step]
            first, end = tiles[0] * depth // PACK, (tiles[-1] + 1) * depth // PACK
            nc.vector.quantize_mx(
                out=codes[:, first:end].bitcast(FP8X4),
                scales=scales[:, first:end],
                in_=made[key, step][:, PACK * first : PACK * end],
            )

        def project(step, a):
            band = steps[step][a] // ROWS
            codes, scales = made["drive_k_q", step]
            bank = psum.tile([P, PACK, P], F32, name="amp", bufs=3)
            for slot in range(PACK):
                for g in range(SRC_PASSES):
                    cols = slice((a * SRC_PASSES + g) * P, (a * SRC_PASSES + g + 1) * P)
                    nc.tensor.matmul_mx(
                        out=bank[:, slot, :],
                        lhsT=made["src_codes", band, slot][:, g, :].bitcast(FP4X4),
                        lhsT_scale=made["src_plane", band][:, g, slot, :],
                        rhs=codes[:, cols].bitcast(FP8X4),
                        rhs_scale=scales[:, cols],
                        start=(g == 0),
                        stop=(g == SRC_PASSES - 1),
                    )
            made["amp", step, a] = bank

        loss_jobs = [(first, end, slot) for first, end in spans for slot in range(PACK)]

        def losses_until(tiles):
            while loss_jobs and loss_jobs[0][0] + (loss_jobs[0][1] - loss_jobs[0][0]) * loss_jobs[0][2] / PACK < tiles:
                first, end, slot = loss_jobs.pop(0)
                band, row = divmod(first, ROWS)
                if slot == 0:
                    made["loss", first] = work.tile([P, PACK, (end - first) * P], F32, name="loss")
                nc.scalar.activation(
                    out=made["loss", first][:, slot, :],
                    in_=dist_rows[:, row * P : (row + end - first) * P],
                    func=EXP,
                    scale=decay_f32[:, band, slot : slot + 1],
                )
                if slot == PACK - 1:
                    for i in range(first, end):
                        made["tile_loss", i] = made["loss", first][:, :, (i - first) * P : (i - first + 1) * P]

        def attenuate(step, a):
            if a == 0:
                shape = [P, len(steps[step]) * M]
                if gpsimd_job(step + 1):
                    far = keep.tile(shape, BF16, name="far_k", tag="far%d" % step, align_bytes=64)
                else:
                    far = work.tile(shape, BF16, name="far_k", align_bytes=64)
                made["far_k", step] = far
            nc.vector.tensor_tensor(
                out=made["far_k", step][:, a * M : (a + 1) * M].rearrange("p (c i t) -> p c t i", i=2, t=PACK),
                in0=made["tile_loss", steps[step][a]].rearrange("p t (c i) -> p c t i", i=2),
                in1=made["amp", step, a][:].rearrange("p t (c i) -> p c t i", i=2),
                op=MULT,
            )

        def receive(step, a):
            band = steps[step][a] // ROWS
            codes, scales = made["far_k_q", step]
            bank = psum.tile([P, Z], F32, name="field")
            cols = slice(a * P, (a + 1) * P)
            nc.tensor.matmul_mx(
                out=bank[:],
                lhsT=codes[:, cols].bitcast(FP8X4),
                lhsT_scale=scales[:, cols],
                rhs=rcv_codes[band].bitcast(FP4X4),
                rhs_scale=rcv_planes[band],
                start=True,
                stop=True,
            )
            made["field", step, a] = bank

        def empty_field(step, a):
            if a == 0:
                made["result", step] = work.tile(
                    [P, len(steps[step]) * Z], F32, name="result", bufs=RESULT_BUFS
                )
            copy_out(
                a > 0 and len(loss_jobs) > 0,
                made["result", step][:, a * Z : (a + 1) * Z],
                made["field", step, a][:],
            )

        def store(step):
            band, row = divmod(steps[step][0], ROWS)
            nc.sync.dma_start(
                out=fields[band, :, row : row + len(steps[step]), :].rearrange("p j z -> p (j z)"),
                in_=made["result", step][:],
            )

        def members(step):
            return range(len(steps[step])) if 0 <= step <= last else range(0)


        nc.scalar.copy(out=dist_f32[:], in_=dist_bf[:])
        spread_dist(0)
        nc.scalar.copy(out=decay_f32[:], in_=decay_bf[:])
        losses_until(PAIR)
        for slot in range(PACK):
            order_codes(0, slot, nc.vector, "first%d" % slot)
        turn_drive(steps[0][0])
        group_drive(0, 0)
        order_scales(0)
        quantize("drive_k", 0, D, [0])
        turn_drive(steps[0][1])
        spread_dist(BANK_CHUNKS)
        group_drive(0, 1)
        project(0, 0)
        quantize("drive_k", 0, D, [1])
        for i in steps[1]:
            turn_drive(i)
        project(0, 1)
        losses_until(2 * PAIR)
        for a in members(0):
            attenuate(0, a)
            group_drive(1, a)
        for i in steps[2]:
            turn_drive(i)
        group_drive(2, 0)
        quantize("drive_k", 1, D, members(1))
        group_drive(2, 1)
        losses_until(LOSS_LEAD)


        for k in range(1, last + 3):
            for a in members(k + 2):
                turn_drive(steps[k + 2][a])
            if members(k + 1):
                quantize("drive_k", k + 1, D, members(k + 1))
            if members(k - 1):
                quantize("far_k", k - 1, M, members(k - 1))
            job = gpsimd_job(k)
            if job:
                order_codes(job[0], job[1], nc.gpsimd, "far%d" % (k - 1))
            for a in members(k - 2):
                empty_field(k - 2, a)
            if members(k - 2):
                store(k - 2)
            for a in members(k + 2):
                group_drive(k + 2, a)
            for a in members(k):
                project(k, a)
            for a in members(k - 1):
                receive(k - 1, a)
            if members(k):
                losses_until(steps[k][-1] + LOSS_LEAD)
            for a in members(k):
                attenuate(k, a)
            if job and job[1] == VECTOR_REORDER_AT:
                order_codes(job[0], 0, nc.vector, "slot0_%d" % job[0])
                order_scales(job[0])
